import numpy as np
CORES = [56,64,184,192,312,320,440,448]
N = 8
C, TIMES = 256, 1
def setup_inputs(rng):
    return {"x": np.exp(rng.standard_normal((N, 128, C), dtype=np.float32))}
def setup_inputs_big(rng):
    d = setup_inputs(rng)
    for k in ("x",): d[k] = (d[k].astype(np.float32) * 1048576.0).astype(d[k].dtype)
    return d
def setup_inputs_small(rng):
    d = setup_inputs(rng)
    for k in ("x",): d[k] = (d[k].astype(np.float32) * (1 / 1048576.0)).astype(d[k].dtype)
    return d
def setup_inputs_mixed(rng):
    d = setup_inputs(rng)
    f = (10.0 ** rng.uniform(-3, 3, (1, 1, C))).astype(np.float32)
    for k in ("x",): d[k] = (d[k].astype(np.float32) * f).astype(d[k].dtype)
    return d
def reference(x):
    X = x.astype(np.float64)
    for _ in range(TIMES):
        X = X / X.sum(axis=2, keepdims=True)
        X = X / X.sum(axis=(0, 1), keepdims=True)
    return {"y": X.astype(np.float32)}

@@ -1,0 +1,170 @@
+from concourse.bass import DstId, RemoteDMATransfer
+from concourse.mybir import AluOpType, AxisListType, ActivationFunctionType
+
+E1 = 8
+E2 = 1
+SIM_CORES = 512
+
+SCRATCH = {
+    "xs": ("sbuf", [128, 256], "float32"),
+    "xn": ("sbuf", [128, 256], "float32"),
+    "ys": ("sbuf", [128, 256], "float32"),
+    "rs": ("sbuf", [128, 1], "float32"),
+    "ri": ("sbuf", [128, 1], "float32"),
+    "v": ("sbuf", [128, 2], "float32"),
+    "one32": ("sbuf", [128, 128], "float32"),
+    "id32": ("sbuf", [128, 128], "float32"),
+    "one16": ("sbuf", [128, 128], "float16"),
+    "eps16": ("sbuf", [128, 128], "float16"),
+    "id16": ("sbuf", [128, 128], "float16"),
+    "sel": ("sbuf", [8, 2], "float32"),
+    "row8": ("sbuf", [8, 128], "float32"),
+    "si32": ("sbuf", [128, 2], "float32"),
+    "hi16": ("sbuf", [128, 2], "float16"),
+    "lo32": ("sbuf", [128, 2], "float32"),
+    "dhi": ("sbuf", [128, 256], "float16"),
+    "dlo": ("sbuf", [128, 256], "float16"),
+    "pss": ("psum", [128, 512], "float32"),
+    "bc0": ("psum", [128, 512], "float32"),
+    "bc1": ("psum", [128, 512], "float32"),
+    "kd": ("dram", [2, 128, 2], "float32"),
+    "dl": ("dram", [4, 128, 2], "float32"),
+}
+SEMAPHORES = ["ld", "c_one", "c_id", "c_k", "s_rs", "s_ri", "s_mm", "s_v", "s_xn", "arr", "lsem", "s_l", "s_S", "s_si",
+              "s_hi", "s_lo", "s_dha", "s_dhb", "s_dla", "s_dlb", "s_b0", "s_b1", "s_y0", "s_y1", "st"]
+
+_PLAN = {}
+
+
+def _low_bits(mask, n):
+    out, b = 0, 1
+    while n > 0:
+        if mask & b:
+            out |= b
+            n -= 1
+        b <<= 1
+    return out
+
+
+def _plan(T, topo):
+    if _PLAN:
+        return _PLAN
+    ranks = list(T.cores)
+    rackp, cablep, helper, serves, feeds = {}, {}, {}, {}, {}
+    for c in ranks:
+        peers = [d for d in ranks if d != c and topo.may_write(c, d)]
+        rackp[c] = [d for d in peers if topo.same_plane(c, d)][0]
+        cablep[c] = [d for d in peers if not topo.same_plane(c, d)][0]
+    for c in ranks:
+        hosts = (topo.host(c), topo.host(cablep[c]))
+        dests = [d for d in ranks if topo.host(d) in hosts]
+        k = [k for k in range(SIM_CORES)
+             if topo.host(k) == topo.host(c) and topo.chip(k) == topo.chip(c) and k not in ranks
+             and topo.die(k) == topo.die(c) and all(topo.may_write(k, d) for d in dests)][0]
+        helper[c] = k
+        serves[k] = [(d, (0 if topo.host(d) == topo.host(c) else 1) + (0 if topo.chip(d) == topo.chip(c) else 2))
+                     for d in dests]
+    for c in ranks:
+        feeds[c] = [(helper[rackp[c]], 1), (helper[c], 0)]
+    _PLAN.update(helper=helper, serves=serves, feeds=feeds)
+    return _PLAN
+
+
+def _send(g, core, topo, pairs, n_eng, srcs, dst_of, sem, lsem):
+    mask = ~0
+    for d, _ in pairs:
+        mask &= topo.mask(core, d)
+    ids = []
+    for d, _ in pairs:
+        rid, pid = topo.addr(d, core)
+        ids.append(DstId(rid=rid, pnc=pid))
+    g.remote_dma_fused([RemoteDMATransfer(dst_ids=ids, dma_engine_mask=_low_bits(mask, n_eng), remote_sem=sem,
+                                          srcs=srcs, dsts=[dst_of(s) for _, s in pairs],
+                                          alu_op=1 if len(srcs) > 1 else 0)], local_sem=lsem)
+
+
+def rank_program(g, core, T, topo):
+    plan = _plan(T, topo)
+    S = T.sem
+    if core in plan["serves"]:
+        g.wait_ge(S.arr, 2 * E1)
+        _send(g, core, topo, plan["serves"][core], E2, [T.kd[0], T.kd[1]], lambda s: T.dl[s], S.arr, S.lsem)
+        g.wait_ge(S.lsem, E2)
+        return
+    if T.rank_of(core) is None:
+        return
+    V, A, P, Q = g.vector, g.scalar, g.tensor, g.sync
+    mult, add, sub = AluOpType.mult, AluOpType.add, AluOpType.subtract
+    X, Copy = AxisListType.X, ActivationFunctionType.Copy
+
+    Q.dma_start(T.xs[:], T.x[:]).then_inc(S.ld, 16)
+
+    V.memset(T.one32[:], 1.0).then_inc(S.c_one, 1)
+    g.wait_ge(S.c_one, 1)
+    g.affine_select(T.id32[:], T.one32[:], [[-1, 128]], AluOpType.is_equal, 0.0, 0, 1).then_inc(S.c_id, 1)
+    V.wait_ge(S.c_one, 1)
+    V.tensor_copy(T.one16[:], T.one32[:]).then_inc(S.c_k, 1)
+    V.tensor_scalar(T.eps16[:], T.one32[:], 2.0 ** -11, None, mult).then_inc(S.c_k, 1)
+    V.wait_ge(S.c_id, 1)
+    V.tensor_copy(T.id16[:], T.id32[:]).then_inc(S.c_k, 1)
+    V.tensor_reduce(T.sel[0:8, 0:1], T.id32[0:8, 0:8:2], X, add).then_inc(S.c_k, 1)
+    V.tensor_reduce(T.sel[0:8, 1:2], T.id32[0:8, 1:8:2], X, add).then_inc(S.c_k, 1)
+
+    V.wait_ge(S.ld, 16)
+    V.tensor_reduce(T.rs[:], T.xs[:], X, add).then_inc(S.s_rs, 1)
+    V.wait_ge(S.s_rs, 1)
+    V.reciprocal(T.ri[:], T.rs[:]).then_inc(S.s_ri, 1)
+    P.wait_ge(S.ld, 16)
+    P.wait_ge(S.s_ri, 1)
+    P.matmul(T.pss[:, 0:1], T.xs[:, 0:256:2], T.ri[:], True, True).then_inc(S.s_mm, 1)
+    P.matmul(T.pss[:, 1:2], T.xs[:, 1:256:2], T.ri[:], True, True).then_inc(S.s_mm, 1)
+    V.wait_ge(S.s_mm, 2)
+    V.tensor_copy(T.v[:], T.pss[:, 0:2]).then_inc(S.s_v, 1)
+    g.wait_ge(S.s_v, 1)
+    _send(g, core, topo, plan["feeds"][core], E1, [T.v[:]], lambda s: T.kd[s], S.arr, S.lsem)
+    A.wait_ge(S.ld, 16)
+    A.wait_ge(S.s_ri, 1)
+    A.activation(T.xn[:], T.xs[:], Copy, scale=T.ri[:]).then_inc(S.s_xn, 1)
+
+    Q.wait_ge(S.arr, 4 * E2)
+    Q.dma_start(T.row8[:], T.dl[:]).then_inc(S.s_l, 16)
+    P.wait_ge(S.c_k, 5)
+    P.wait_ge(S.s_v, 1)
+    P.wait_ge(S.s_l, 16)
+    P.matmul(T.pss[:, 2:4], T.row8[:], T.sel[:], True, True).then_inc(S.s_S, 1)
+    V.wait_ge(S.s_S, 1)
+    V.reciprocal(T.si32[:], T.pss[:, 2:4]).then_inc(S.s_si, 1)
+
+    A.wait_ge(S.c_k, 5)
+    A.wait_ge(S.s_si, 1)
+    A.activation(T.dhi[:, 0:128], T.id16[:], Copy, scale=T.si32[:, 0:1]).then_inc(S.s_dha, 1)
+    A.activation(T.dhi[:, 128:256], T.id16[:], Copy, scale=T.si32[:, 1:2]).then_inc(S.s_dhb, 1)
+    V.wait_ge(S.c_k, 5)
+    V.wait_ge(S.s_si, 1)
+    V.tensor_copy(T.hi16[:], T.si32[:]).then_inc(S.s_hi, 1)
+    V.wait_ge(S.s_hi, 1)
+    V.tensor_tensor(T.lo32[:], T.si32[:], T.hi16[:], sub).then_inc(S.s_lo, 1)
+    V.wait_ge(S.s_lo, 1)
+    V.tensor_scalar(T.dlo[:, 0:128], T.id16[:], T.lo32[:, 0:1], 2048.0, mult, mult).then_inc(S.s_dla, 1)
+    V.tensor_scalar(T.dlo[:, 128:256], T.id16[:], T.lo32[:, 1:2], 2048.0, mult, mult).then_inc(S.s_dlb, 1)
+
+    P.wait_ge(S.s_dha, 1)
+    P.matmul(T.bc0[:, 0:128], T.one16[:], T.dhi[:, 0:128], True, False)
+    P.wait_ge(S.s_dla, 1)
+    P.matmul(T.bc0[:, 0:128], T.eps16[:], T.dlo[:, 0:128], False, True).then_inc(S.s_b0, 1)
+    P.wait_ge(S.s_dhb, 1)
+    P.matmul(T.bc1[:, 0:128], T.one16[:], T.dhi[:, 128:256], True, False)
+    P.wait_ge(S.s_dlb, 1)
+    P.matmul(T.bc1[:, 0:128], T.eps16[:], T.dlo[:, 128:256], False, True).then_inc(S.s_b1, 1)
+
+    V.wait_ge(S.s_xn, 1)
+    V.wait_ge(S.s_b0, 1)
+    V.tensor_tensor(T.ys[:, 0:128], T.xn[:, 0:128], T.bc0[:, 0:128], mult).then_inc(S.s_y0, 1)
+    V.wait_ge(S.s_b1, 1)
+    V.tensor_tensor(T.ys[:, 128:256], T.xn[:, 128:256], T.bc1[:, 0:128], mult).then_inc(S.s_y1, 1)
+    Q.wait_ge(S.s_y0, 1)
+    Q.dma_start(T.y[:, 0:128], T.ys[:, 0:128]).then_inc(S.st, 16)
+    A.wait_ge(S.s_y1, 1)
+    A.dma_start(T.y[:, 128:256], T.ys[:, 128:256]).then_inc(S.st, 16)
+    g.wait_ge(S.lsem, E1)
+    g.wait_ge(S.st, 32)

@@ -1,8 +1,7 @@
 from concourse.bass import DstId, RemoteDMATransfer
 from concourse.mybir import AluOpType, AxisListType, ActivationFunctionType
 
-E1 = 8
-E2 = 1
+E = 8
 SIM_CORES = 512
 
 SCRATCH = {
@@ -11,14 +10,15 @@ SCRATCH = {
     "ys": ("sbuf", [128, 256], "float32"),
     "rs": ("sbuf", [128, 1], "float32"),
     "ri": ("sbuf", [128, 1], "float32"),
-    "v": ("sbuf", [128, 2], "float32"),
     "one32": ("sbuf", [128, 128], "float32"),
     "id32": ("sbuf", [128, 128], "float32"),
     "one16": ("sbuf", [128, 128], "float16"),
     "eps16": ("sbuf", [128, 128], "float16"),
     "id16": ("sbuf", [128, 128], "float16"),
-    "sel": ("sbuf", [8, 2], "float32"),
-    "row8": ("sbuf", [8, 128], "float32"),
+    "kin": ("sbuf", [128, 4], "float32"),
+    "sumb": ("sbuf", [128, 16], "float32"),
+    "junk": ("sbuf", [128, 8], "float32"),
+    "s2": ("sbuf", [128, 2], "float32"),
     "si32": ("sbuf", [128, 2], "float32"),
     "hi16": ("sbuf", [128, 2], "float16"),
     "lo32": ("sbuf", [128, 2], "float32"),
@@ -27,10 +27,8 @@ SCRATCH = {
     "pss": ("psum", [128, 512], "float32"),
     "bc0": ("psum", [128, 512], "float32"),
     "bc1": ("psum", [128, 512], "float32"),
-    "kd": ("dram", [2, 128, 2], "float32"),
-    "dl": ("dram", [4, 128, 2], "float32"),
 }
-SEMAPHORES = ["ld", "c_one", "c_id", "c_k", "s_rs", "s_ri", "s_mm", "s_v", "s_xn", "arr", "lsem", "s_l", "s_S", "s_si",
+SEMAPHORES = ["ld", "c_one", "c_id", "c_k", "s_rs", "s_ri", "s_mm", "s_v", "s_xn", "arr", "a_rp", "lsem", "s_S", "s_si",
               "s_hi", "s_lo", "s_dha", "s_dhb", "s_dla", "s_dlb", "s_b0", "s_b1", "s_y0", "s_y1", "st"]
 
 _PLAN = {}
@@ -57,58 +55,58 @@ def _plan(T, topo):
         cablep[c] = [d for d in peers if not topo.same_plane(c, d)][0]
     for c in ranks:
         hosts = (topo.host(c), topo.host(cablep[c]))
-        dests = [d for d in ranks if topo.host(d) in hosts]
+        dests = [d for d in ranks if topo.host(d) in hosts and not topo.may_write(c, d) and d != c]
         k = [k for k in range(SIM_CORES)
              if topo.host(k) == topo.host(c) and topo.chip(k) == topo.chip(c) and k not in ranks
              and topo.die(k) == topo.die(c) and all(topo.may_write(k, d) for d in dests)][0]
         helper[c] = k
-        serves[k] = [(d, (0 if topo.host(d) == topo.host(c) else 1) + (0 if topo.chip(d) == topo.chip(c) else 2))
-                     for d in dests]
+        serves[k] = [(d, 0 if topo.host(d) == topo.host(c) else 1) for d in dests]
+        serves[k].sort(key=lambda p: -p[1])
     for c in ranks:
         feeds[c] = [(helper[rackp[c]], 1), (helper[c], 0)]
-    _PLAN.update(helper=helper, serves=serves, feeds=feeds)
+    _PLAN.update(rackp=rackp, cablep=cablep, serves=serves, feeds=feeds)
     return _PLAN
 
 
-def _send(g, core, topo, pairs, n_eng, srcs, dst_of, sem, lsem):
+def _send(g, core, topo, dests, srcs, dsts, sem, lsem):
     mask = ~0
-    for d, _ in pairs:
-        mask &= topo.mask(core, d)
     ids = []
-    for d, _ in pairs:
+    for d in dests:
+        mask &= topo.mask(core, d)
         rid, pid = topo.addr(d, core)
         ids.append(DstId(rid=rid, pnc=pid))
-    g.remote_dma_fused([RemoteDMATransfer(dst_ids=ids, dma_engine_mask=_low_bits(mask, n_eng), remote_sem=sem,
-                                          srcs=srcs, dsts=[dst_of(s) for _, s in pairs],
-                                          alu_op=1 if len(srcs) > 1 else 0)], local_sem=lsem)
+    g.remote_dma_fused([RemoteDMATransfer(dst_ids=ids, dma_engine_mask=_low_bits(mask, E), remote_sem=sem,
+                                          srcs=srcs, dsts=dsts, alu_op=1 if len(srcs) > 1 else 0)], local_sem=lsem)
 
 
 def rank_program(g, core, T, topo):
     plan = _plan(T, topo)
     S = T.sem
     if core in plan["serves"]:
-        g.wait_ge(S.arr, 2 * E1)
-        _send(g, core, topo, plan["serves"][core], E2, [T.kd[0], T.kd[1]], lambda s: T.dl[s], S.arr, S.lsem)
-        g.wait_ge(S.lsem, E2)
+        pairs = plan["serves"][core]
+        g.wait_ge(S.arr, 2 * E)
+        _send(g, core, topo, [d for d, _ in pairs], [T.kin[:]], [T.sumb[:, 4 * s:4 * s + 4] for _, s in pairs],
+              S.arr, S.lsem)
+        g.wait_ge(S.lsem, E)
         return
     if T.rank_of(core) is None:
         return
     V, A, P, Q = g.vector, g.scalar, g.tensor, g.sync
     mult, add, sub = AluOpType.mult, AluOpType.add, AluOpType.subtract
     X, Copy = AxisListType.X, ActivationFunctionType.Copy
+    own, from_rp, from_cp = T.sumb[:, 12:14], T.sumb[:, 8:10], T.sumb[:, 10:12]
 
     Q.dma_start(T.xs[:], T.x[:]).then_inc(S.ld, 16)
 
     V.memset(T.one32[:], 1.0).then_inc(S.c_one, 1)
     g.wait_ge(S.c_one, 1)
     g.affine_select(T.id32[:], T.one32[:], [[-1, 128]], AluOpType.is_equal, 0.0, 0, 1).then_inc(S.c_id, 1)
+    V.memset(T.sumb[:, 14:16], 0.0).then_inc(S.c_k, 1)
     V.wait_ge(S.c_one, 1)
     V.tensor_copy(T.one16[:], T.one32[:]).then_inc(S.c_k, 1)
     V.tensor_scalar(T.eps16[:], T.one32[:], 2.0 ** -11, None, mult).then_inc(S.c_k, 1)
     V.wait_ge(S.c_id, 1)
     V.tensor_copy(T.id16[:], T.id32[:]).then_inc(S.c_k, 1)
-    V.tensor_reduce(T.sel[0:8, 0:1], T.id32[0:8, 0:8:2], X, add).then_inc(S.c_k, 1)
-    V.tensor_reduce(T.sel[0:8, 1:2], T.id32[0:8, 1:8:2], X, add).then_inc(S.c_k, 1)
 
     V.wait_ge(S.ld, 16)
     V.tensor_reduce(T.rs[:], T.xs[:], X, add).then_inc(S.s_rs, 1)
@@ -116,31 +114,39 @@ def rank_program(g, core, T, topo):
     V.reciprocal(T.ri[:], T.rs[:]).then_inc(S.s_ri, 1)
     P.wait_ge(S.ld, 16)
     P.wait_ge(S.s_ri, 1)
-    P.matmul(T.pss[:, 0:1], T.xs[:, 0:256:2], T.ri[:], True, True).then_inc(S.s_mm, 1)
-    P.matmul(T.pss[:, 1:2], T.xs[:, 1:256:2], T.ri[:], True, True).then_inc(S.s_mm, 1)
+    P.matmul(T.pss[:, 0:1], T.xs[:, 0:128], T.ri[:], True, True).then_inc(S.s_mm, 1)
+    P.matmul(T.pss[:, 1:2], T.xs[:, 128:256], T.ri[:], True, True).then_inc(S.s_mm, 1)
     V.wait_ge(S.s_mm, 2)
-    V.tensor_copy(T.v[:], T.pss[:, 0:2]).then_inc(S.s_v, 1)
+    V.tensor_copy(own, T.pss[:, 0:2]).then_inc(S.s_v, 1)
+
     g.wait_ge(S.s_v, 1)
-    _send(g, core, topo, plan["feeds"][core], E1, [T.v[:]], lambda s: T.kd[s], S.arr, S.lsem)
+    feeds = plan["feeds"][core]
+    _send(g, core, topo, [k for k, _ in feeds], [own], [T.kin[:, 2 * s:2 * s + 2] for _, s in feeds], S.arr, S.lsem)
+    _send(g, core, topo, [plan["rackp"][core]], [own], [from_rp], S.a_rp, S.lsem)
+    g.wait_ge(S.a_rp, E)
+    _send(g, core, topo, [plan["cablep"][core]], [own, from_rp], [from_cp], S.arr, S.lsem)
+
     A.wait_ge(S.ld, 16)
     A.wait_ge(S.s_ri, 1)
     A.activation(T.xn[:], T.xs[:], Copy, scale=T.ri[:]).then_inc(S.s_xn, 1)
 
-    Q.wait_ge(S.arr, 4 * E2)
-    Q.dma_start(T.row8[:], T.dl[:]).then_inc(S.s_l, 16)
-    P.wait_ge(S.c_k, 5)
-    P.wait_ge(S.s_v, 1)
-    P.wait_ge(S.s_l, 16)
-    P.matmul(T.pss[:, 2:4], T.row8[:], T.sel[:], True, True).then_inc(S.s_S, 1)
-    V.wait_ge(S.s_S, 1)
-    V.reciprocal(T.si32[:], T.pss[:, 2:4]).then_inc(S.s_si, 1)
+    V.wait_ge(S.c_k, 4)
+    V.wait_ge(S.s_v, 1)
+    V.wait_ge(S.a_rp, E)
+    V.wait_ge(S.arr, 3 * E)
+    V.tensor_reduce(T.s2[:, 0:1], T.sumb[:, 0:16:2], X, add).then_inc(S.s_S, 1)
+    A.wait_ge(S.c_k, 4)
+    A.wait_ge(S.s_v, 1)
+    A.wait_ge(S.a_rp, E)
+    A.wait_ge(S.arr, 3 * E)
+    A.activation(T.junk[:], T.sumb[:, 1:16:2], Copy, accum_out=T.s2[:, 1:2]).then_inc(S.s_S, 1)
+    V.wait_ge(S.s_S, 2)
+    V.reciprocal(T.si32[:], T.s2[:]).then_inc(S.s_si, 1)
 
-    A.wait_ge(S.c_k, 5)
-    A.wait_ge(S.s_si, 1)
-    A.activation(T.dhi[:, 0:128], T.id16[:], Copy, scale=T.si32[:, 0:1]).then_inc(S.s_dha, 1)
-    A.activation(T.dhi[:, 128:256], T.id16[:], Copy, scale=T.si32[:, 1:2]).then_inc(S.s_dhb, 1)
-    V.wait_ge(S.c_k, 5)
     V.wait_ge(S.s_si, 1)
+    V.tensor_scalar(T.dhi[:, 0:128], T.id16[:], T.si32[:, 0:1], None, mult).then_inc(S.s_dha, 1)
+    A.wait_ge(S.s_si, 1)
+    A.activation(T.dhi[:, 128:256], T.id16[:], Copy, scale=T.si32[:, 1:2]).then_inc(S.s_dhb, 1)
     V.tensor_copy(T.hi16[:], T.si32[:]).then_inc(S.s_hi, 1)
     V.wait_ge(S.s_hi, 1)
     V.tensor_tensor(T.lo32[:], T.si32[:], T.hi16[:], sub).then_inc(S.s_lo, 1)
@@ -148,12 +154,13 @@ def rank_program(g, core, T, topo):
     V.tensor_scalar(T.dlo[:, 0:128], T.id16[:], T.lo32[:, 0:1], 2048.0, mult, mult).then_inc(S.s_dla, 1)
     V.tensor_scalar(T.dlo[:, 128:256], T.id16[:], T.lo32[:, 1:2], 2048.0, mult, mult).then_inc(S.s_dlb, 1)
 
+    P.wait_ge(S.c_k, 4)
     P.wait_ge(S.s_dha, 1)
     P.matmul(T.bc0[:, 0:128], T.one16[:], T.dhi[:, 0:128], True, False)
-    P.wait_ge(S.s_dla, 1)
-    P.matmul(T.bc0[:, 0:128], T.eps16[:], T.dlo[:, 0:128], False, True).then_inc(S.s_b0, 1)
     P.wait_ge(S.s_dhb, 1)
     P.matmul(T.bc1[:, 0:128], T.one16[:], T.dhi[:, 128:256], True, False)
+    P.wait_ge(S.s_dla, 1)
+    P.matmul(T.bc0[:, 0:128], T.eps16[:], T.dlo[:, 0:128], False, True).then_inc(S.s_b0, 1)
     P.wait_ge(S.s_dlb, 1)
     P.matmul(T.bc1[:, 0:128], T.eps16[:], T.dlo[:, 128:256], False, True).then_inc(S.s_b1, 1)
 
@@ -166,5 +173,5 @@ def rank_program(g, core, T, topo):
     Q.dma_start(T.y[:, 0:128], T.ys[:, 0:128]).then_inc(S.st, 16)
     A.wait_ge(S.s_y1, 1)
     A.dma_start(T.y[:, 128:256], T.ys[:, 128:256]).then_inc(S.st, 16)
-    g.wait_ge(S.lsem, E1)
+    g.wait_ge(S.lsem, 3 * E)
     g.wait_ge(S.st, 32)

@@ -12,7 +12,7 @@ SCRATCH = {
     "ri": ("sbuf", [128, 1], "float32"),
     "one32": ("sbuf", [128, 128], "float32"),
     "id32": ("sbuf", [128, 128], "float32"),
-    "one16": ("sbuf", [128, 128], "float16"),
+    "c16": ("sbuf", [128, 128], "float16"),
     "eps16": ("sbuf", [128, 128], "float16"),
     "id16": ("sbuf", [128, 128], "float16"),
     "kin": ("sbuf", [128, 4], "float32"),
@@ -28,8 +28,8 @@ SCRATCH = {
     "bc0": ("psum", [128, 512], "float32"),
     "bc1": ("psum", [128, 512], "float32"),
 }
-SEMAPHORES = ["ld", "c_one", "c_id", "c_k", "s_rs", "s_ri", "s_mm", "s_v", "s_xn", "arr", "a_rp", "lsem", "s_S", "s_si",
-              "s_hi", "s_lo", "s_dha", "s_dhb", "s_dla", "s_dlb", "s_b0", "s_b1", "s_y0", "s_y1", "st"]
+SEMAPHORES = ["ld", "c_one", "c_id", "c_k", "c_idr", "s_rs", "s_ri", "s_mm", "s_v", "s_xn", "arr", "a_rp", "lsem",
+              "s_S", "s_si", "s_hi", "s_lo", "s_dha", "s_dhb", "s_dla", "s_dlb", "s_b0", "s_b1", "s_y0", "s_y1", "st"]
 
 _PLAN = {}
 
@@ -48,65 +48,77 @@ def _plan(T, topo):
     if _PLAN:
         return _PLAN
     ranks = list(T.cores)
-    rackp, cablep, helper, serves, feeds = {}, {}, {}, {}, {}
+    rackp, cablep, helper, owner, serves = {}, {}, {}, {}, {}
     for c in ranks:
         peers = [d for d in ranks if d != c and topo.may_write(c, d)]
         rackp[c] = [d for d in peers if topo.same_plane(c, d)][0]
         cablep[c] = [d for d in peers if not topo.same_plane(c, d)][0]
     for c in ranks:
-        hosts = (topo.host(c), topo.host(cablep[c]))
+        hosts = (topo.host(c), topo.host(rackp[c]))
         dests = [d for d in ranks if topo.host(d) in hosts and not topo.may_write(c, d) and d != c]
         k = [k for k in range(SIM_CORES)
              if topo.host(k) == topo.host(c) and topo.chip(k) == topo.chip(c) and k not in ranks
              and topo.die(k) == topo.die(c) and all(topo.may_write(k, d) for d in dests)][0]
         helper[c] = k
+        owner[k] = c
         serves[k] = [(d, 0 if topo.host(d) == topo.host(c) else 1) for d in dests]
-        serves[k].sort(key=lambda p: -p[1])
-    for c in ranks:
-        feeds[c] = [(helper[rackp[c]], 1), (helper[c], 0)]
-    _PLAN.update(rackp=rackp, cablep=cablep, serves=serves, feeds=feeds)
+    _PLAN.update(rackp=rackp, cablep=cablep, helper=helper, owner=owner, serves=serves)
     return _PLAN
 
 
-def _send(g, core, topo, dests, srcs, dsts, sem, lsem):
-    mask = ~0
+def _transfer(core, topo, mask, dests, srcs, dsts, sem):
     ids = []
     for d in dests:
-        mask &= topo.mask(core, d)
         rid, pid = topo.addr(d, core)
         ids.append(DstId(rid=rid, pnc=pid))
-    g.remote_dma_fused([RemoteDMATransfer(dst_ids=ids, dma_engine_mask=_low_bits(mask, E), remote_sem=sem,
-                                          srcs=srcs, dsts=dsts, alu_op=1 if len(srcs) > 1 else 0)], local_sem=lsem)
+    return RemoteDMATransfer(dst_ids=ids, dma_engine_mask=mask, remote_sem=sem, srcs=srcs, dsts=dsts,
+                             alu_op=1 if len(srcs) > 1 else 0)
 
 
 def rank_program(g, core, T, topo):
     plan = _plan(T, topo)
     S = T.sem
-    if core in plan["serves"]:
-        pairs = plan["serves"][core]
-        g.wait_ge(S.arr, 2 * E)
-        _send(g, core, topo, [d for d, _ in pairs], [T.kin[:]], [T.sumb[:, 4 * s:4 * s + 4] for _, s in pairs],
-              S.arr, S.lsem)
-        g.wait_ge(S.lsem, E)
-        return
-    if T.rank_of(core) is None:
-        return
     V, A, P, Q = g.vector, g.scalar, g.tensor, g.sync
     mult, add, sub = AluOpType.mult, AluOpType.add, AluOpType.subtract
     X, Copy = AxisListType.X, ActivationFunctionType.Copy
+
+    if core in plan["serves"]:
+        pairs = plan["serves"][core]
+        own_rank = plan["owner"][core]
+        far = topo.mask(core, own_rank)
+        for d, _ in pairs:
+            far &= topo.mask(core, d)
+        far = _low_bits(far, E)
+        V.memset(T.one32[:], 1.0).then_inc(S.c_one, 1)
+        g.wait_ge(S.c_one, 1)
+        g.affine_select(T.id32[:], T.one32[:], [[-1, 128]], AluOpType.is_equal, 0.0, 0, 1).then_inc(S.c_id, 1)
+        V.wait_ge(S.c_id, 1)
+        V.tensor_copy(T.id16[:], T.id32[:]).then_inc(S.c_k, 1)
+        g.wait_ge(S.c_k, 1)
+        g.remote_dma_fused([_transfer(core, topo, far, [own_rank], [T.id16[:]], [T.id16[:]], S.c_idr)],
+                           local_sem=S.lsem)
+        g.wait_ge(S.arr, E)
+        g.wait_ge(S.a_rp, E)
+        g.remote_dma_fused([_transfer(core, topo, far, [d for d, _ in pairs], [T.kin[:]],
+                                      [T.sumb[:, 4 * s:4 * s + 4] for _, s in pairs], S.arr)], local_sem=S.lsem)
+        g.wait_ge(S.lsem, 2 * E)
+        return
+    if T.rank_of(core) is None:
+        return
     own, from_rp, from_cp = T.sumb[:, 12:14], T.sumb[:, 8:10], T.sumb[:, 10:12]
+    my_helper, rackp, cablep = plan["helper"][core], plan["rackp"][core], plan["cablep"][core]
+    cable_helper = plan["helper"][cablep]
+    far = topo.mask(core, cable_helper) & topo.mask(core, rackp) & topo.mask(core, cablep)
+    near = _low_bits(topo.mask(core, my_helper) & ~far, E)
+    far = _low_bits(far, E)
 
     Q.dma_start(T.xs[:], T.x[:]).then_inc(S.ld, 16)
 
     V.memset(T.one32[:], 1.0).then_inc(S.c_one, 1)
-    g.wait_ge(S.c_one, 1)
-    g.affine_select(T.id32[:], T.one32[:], [[-1, 128]], AluOpType.is_equal, 0.0, 0, 1).then_inc(S.c_id, 1)
     V.memset(T.sumb[:, 14:16], 0.0).then_inc(S.c_k, 1)
     V.wait_ge(S.c_one, 1)
-    V.tensor_copy(T.one16[:], T.one32[:]).then_inc(S.c_k, 1)
-    V.tensor_scalar(T.eps16[:], T.one32[:], 2.0 ** -11, None, mult).then_inc(S.c_k, 1)
-    V.wait_ge(S.c_id, 1)
-    V.tensor_copy(T.id16[:], T.id32[:]).then_inc(S.c_k, 1)
+    V.tensor_scalar(T.c16[:], T.one32[:], 16.0, None, mult).then_inc(S.c_k, 1)
+    V.tensor_scalar(T.eps16[:], T.one32[:], 2.0 ** -7, None, mult).then_inc(S.c_k, 1)
 
     V.wait_ge(S.ld, 16)
     V.tensor_reduce(T.rs[:], T.xs[:], X, add).then_inc(S.s_rs, 1)
@@ -117,25 +129,27 @@ def rank_program(g, core, T, topo):
     P.matmul(T.pss[:, 0:1], T.xs[:, 0:128], T.ri[:], True, True).then_inc(S.s_mm, 1)
     P.matmul(T.pss[:, 1:2], T.xs[:, 128:256], T.ri[:], True, True).then_inc(S.s_mm, 1)
     V.wait_ge(S.s_mm, 2)
-    V.tensor_copy(own, T.pss[:, 0:2]).then_inc(S.s_v, 1)
+    V.tensor_scalar(own, T.pss[:, 0:2], 16.0, None, mult).then_inc(S.s_v, 1)
 
     g.wait_ge(S.s_v, 1)
-    feeds = plan["feeds"][core]
-    _send(g, core, topo, [k for k, _ in feeds], [own], [T.kin[:, 2 * s:2 * s + 2] for _, s in feeds], S.arr, S.lsem)
-    _send(g, core, topo, [plan["rackp"][core]], [own], [from_rp], S.a_rp, S.lsem)
+    g.remote_dma_fused([_transfer(core, topo, near, [my_helper], [own], [T.kin[:, 0:2]], S.arr),
+                        _transfer(core, topo, far, [cable_helper, rackp], [own], [T.kin[:, 2:4], from_rp], S.a_rp)],
+                       local_sem=S.lsem)
     g.wait_ge(S.a_rp, E)
-    _send(g, core, topo, [plan["cablep"][core]], [own, from_rp], [from_cp], S.arr, S.lsem)
+    g.remote_dma_fused([_transfer(core, topo, far, [cablep], [own, from_rp], [from_cp], S.arr)], local_sem=S.lsem)
 
     A.wait_ge(S.ld, 16)
     A.wait_ge(S.s_ri, 1)
     A.activation(T.xn[:], T.xs[:], Copy, scale=T.ri[:]).then_inc(S.s_xn, 1)
 
-    V.wait_ge(S.c_k, 4)
+    V.wait_ge(S.c_k, 3)
+    V.wait_ge(S.c_idr, E)
     V.wait_ge(S.s_v, 1)
     V.wait_ge(S.a_rp, E)
     V.wait_ge(S.arr, 3 * E)
     V.tensor_reduce(T.s2[:, 0:1], T.sumb[:, 0:16:2], X, add).then_inc(S.s_S, 1)
-    A.wait_ge(S.c_k, 4)
+    A.wait_ge(S.c_k, 3)
+    A.wait_ge(S.c_idr, E)
     A.wait_ge(S.s_v, 1)
     A.wait_ge(S.a_rp, E)
     A.wait_ge(S.arr, 3 * E)
@@ -154,11 +168,11 @@ def rank_program(g, core, T, topo):
     V.tensor_scalar(T.dlo[:, 0:128], T.id16[:], T.lo32[:, 0:1], 2048.0, mult, mult).then_inc(S.s_dla, 1)
     V.tensor_scalar(T.dlo[:, 128:256], T.id16[:], T.lo32[:, 1:2], 2048.0, mult, mult).then_inc(S.s_dlb, 1)
 
-    P.wait_ge(S.c_k, 4)
+    P.wait_ge(S.c_k, 3)
     P.wait_ge(S.s_dha, 1)
-    P.matmul(T.bc0[:, 0:128], T.one16[:], T.dhi[:, 0:128], True, False)
+    P.matmul(T.bc0[:, 0:128], T.c16[:], T.dhi[:, 0:128], True, False)
     P.wait_ge(S.s_dhb, 1)
-    P.matmul(T.bc1[:, 0:128], T.one16[:], T.dhi[:, 128:256], True, False)
+    P.matmul(T.bc1[:, 0:128], T.c16[:], T.dhi[:, 128:256], True, False)
     P.wait_ge(S.s_dla, 1)
     P.matmul(T.bc0[:, 0:128], T.eps16[:], T.dlo[:, 0:128], False, True).then_inc(S.s_b0, 1)
     P.wait_ge(S.s_dlb, 1)

@@ -11,10 +11,12 @@ SCRATCH = {
     "rs": ("sbuf", [128, 1], "float32"),
     "ri": ("sbuf", [128, 1], "float32"),
     "one32": ("sbuf", [128, 128], "float32"),
-    "id32": ("sbuf", [128, 128], "float32"),
+    "oneb": ("sbuf", [128, 128], "bfloat16"),
+    "idm": ("sbuf", [128, 128], "bfloat16"),
+    "idh": ("sbuf", [128, 64], "bfloat16"),
+    "idr": ("sbuf", [128, 128], "bfloat16"),
     "c16": ("sbuf", [128, 128], "float16"),
     "eps16": ("sbuf", [128, 128], "float16"),
-    "id16": ("sbuf", [128, 128], "float16"),
     "kin": ("sbuf", [128, 4], "float32"),
     "sumb": ("sbuf", [128, 16], "float32"),
     "junk": ("sbuf", [128, 8], "float32"),
@@ -27,9 +29,12 @@ SCRATCH = {
     "pss": ("psum", [128, 512], "float32"),
     "bc0": ("psum", [128, 512], "float32"),
     "bc1": ("psum", [128, 512], "float32"),
+    "bc2": ("psum", [128, 512], "float32"),
+    "bc3": ("psum", [128, 512], "float32"),
 }
-SEMAPHORES = ["ld", "c_one", "c_id", "c_k", "c_idr", "s_rs", "s_ri", "s_mm", "s_v", "s_xn", "arr", "a_rp", "lsem",
-              "s_S", "s_si", "s_hi", "s_lo", "s_dha", "s_dhb", "s_dla", "s_dlb", "s_b0", "s_b1", "s_y0", "s_y1", "st"]
+SEMAPHORES = ["ld", "c_one", "c_ob", "c_id", "c_k", "c_idh", "c_idr", "s_rs", "s_ri", "s_mm", "s_v", "s_xn", "arr",
+              "a_rp", "lsem", "s_S", "s_si", "s_hi", "s_lo", "s_dha", "s_dhb", "s_dla", "s_dlb", "s_b0", "s_b1",
+              "s_b2", "s_b3", "s_y0", "s_y1", "st"]
 
 _PLAN = {}
 
@@ -48,7 +53,7 @@ def _plan(T, topo):
     if _PLAN:
         return _PLAN
     ranks = list(T.cores)
-    rackp, cablep, helper, owner, serves = {}, {}, {}, {}, {}
+    rackp, cablep, helper, serves = {}, {}, {}, {}
     for c in ranks:
         peers = [d for d in ranks if d != c and topo.may_write(c, d)]
         rackp[c] = [d for d in peers if topo.same_plane(c, d)][0]
@@ -60,9 +65,8 @@ def _plan(T, topo):
              if topo.host(k) == topo.host(c) and topo.chip(k) == topo.chip(c) and k not in ranks
              and topo.die(k) == topo.die(c) and all(topo.may_write(k, d) for d in dests)][0]
         helper[c] = k
-        owner[k] = c
         serves[k] = [(d, 0 if topo.host(d) == topo.host(c) else 1) for d in dests]
-    _PLAN.update(rackp=rackp, cablep=cablep, helper=helper, owner=owner, serves=serves)
+    _PLAN.update(rackp=rackp, cablep=cablep, helper=helper, serves=serves)
     return _PLAN
 
 
@@ -84,23 +88,17 @@ def rank_program(g, core, T, topo):
 
     if core in plan["serves"]:
         pairs = plan["serves"][core]
-        own_rank = plan["owner"][core]
-        far = topo.mask(core, own_rank)
+        far = ~0
         for d, _ in pairs:
             far &= topo.mask(core, d)
         far = _low_bits(far, E)
-        V.memset(T.one32[:], 1.0).then_inc(S.c_one, 1)
-        g.wait_ge(S.c_one, 1)
-        g.affine_select(T.id32[:], T.one32[:], [[-1, 128]], AluOpType.is_equal, 0.0, 0, 1).then_inc(S.c_id, 1)
-        V.wait_ge(S.c_id, 1)
-        V.tensor_copy(T.id16[:], T.id32[:]).then_inc(S.c_k, 1)
-        g.wait_ge(S.c_k, 1)
-        g.remote_dma_fused([_transfer(core, topo, far, [own_rank], [T.id16[:]], [T.id16[:]], S.c_idr)],
-                           local_sem=S.lsem)
+        g.wait_ge(S.c_idh, E)
+        g.remote_dma_fused([_transfer(core, topo, far, [d for d, sl in pairs if sl == 0], [T.idh[:]],
+                                      [T.idr[:, 0:64]], S.c_idr)], local_sem=S.lsem)
         g.wait_ge(S.arr, E)
         g.wait_ge(S.a_rp, E)
         g.remote_dma_fused([_transfer(core, topo, far, [d for d, _ in pairs], [T.kin[:]],
-                                      [T.sumb[:, 4 * s:4 * s + 4] for _, s in pairs], S.arr)], local_sem=S.lsem)
+                                      [T.sumb[:, 4 * sl:4 * sl + 4] for _, sl in pairs], S.arr)], local_sem=S.lsem)
         g.wait_ge(S.lsem, 2 * E)
         return
     if T.rank_of(core) is None:
@@ -114,6 +112,13 @@ def rank_program(g, core, T, topo):
 
     Q.dma_start(T.xs[:], T.x[:]).then_inc(S.ld, 16)
 
+    V.memset(T.oneb[:], 1.0).then_inc(S.c_ob, 1)
+    g.wait_ge(S.c_ob, 1)
+    g.affine_select(T.idm[:], T.oneb[:], [[-1, 128]], AluOpType.is_equal, 0.0, 0, 1).then_inc(S.c_id, 1)
+    g.wait_ge(S.c_id, 1)
+    g.remote_dma_fused([_transfer(core, topo, near, [my_helper], [T.idm[:, 0:64]], [T.idh[:]], S.c_idh),
+                        _transfer(core, topo, far, [rackp], [T.idm[:, 64:128]], [T.idr[:, 64:128]], S.c_idr)],
+                       local_sem=S.lsem)
     V.memset(T.one32[:], 1.0).then_inc(S.c_one, 1)
     V.memset(T.sumb[:, 14:16], 0.0).then_inc(S.c_k, 1)
     V.wait_ge(S.c_one, 1)
@@ -143,13 +148,13 @@ def rank_program(g, core, T, topo):
     A.activation(T.xn[:], T.xs[:], Copy, scale=T.ri[:]).then_inc(S.s_xn, 1)
 
     V.wait_ge(S.c_k, 3)
-    V.wait_ge(S.c_idr, E)
+    V.wait_ge(S.c_idr, 2 * E)
     V.wait_ge(S.s_v, 1)
     V.wait_ge(S.a_rp, E)
     V.wait_ge(S.arr, 3 * E)
     V.tensor_reduce(T.s2[:, 0:1], T.sumb[:, 0:16:2], X, add).then_inc(S.s_S, 1)
     A.wait_ge(S.c_k, 3)
-    A.wait_ge(S.c_idr, E)
+    A.wait_ge(S.c_idr, 2 * E)
     A.wait_ge(S.s_v, 1)
     A.wait_ge(S.a_rp, E)
     A.wait_ge(S.arr, 3 * E)
@@ -158,34 +163,47 @@ def rank_program(g, core, T, topo):
     V.reciprocal(T.si32[:], T.s2[:]).then_inc(S.s_si, 1)
 
     V.wait_ge(S.s_si, 1)
-    V.tensor_scalar(T.dhi[:, 0:128], T.id16[:], T.si32[:, 0:1], None, mult).then_inc(S.s_dha, 1)
+    V.tensor_scalar(T.dhi[:, 0:128], T.idr[:], T.si32[:, 0:1], None, mult).then_inc(S.s_dha, 1)
     A.wait_ge(S.s_si, 1)
-    A.activation(T.dhi[:, 128:256], T.id16[:], Copy, scale=T.si32[:, 1:2]).then_inc(S.s_dhb, 1)
+    A.activation(T.dhi[:, 128:256], T.idr[:], Copy, scale=T.si32[:, 1:2]).then_inc(S.s_dhb, 1)
     V.tensor_copy(T.hi16[:], T.si32[:]).then_inc(S.s_hi, 1)
     V.wait_ge(S.s_hi, 1)
     V.tensor_tensor(T.lo32[:], T.si32[:], T.hi16[:], sub).then_inc(S.s_lo, 1)
     V.wait_ge(S.s_lo, 1)
-    V.tensor_scalar(T.dlo[:, 0:128], T.id16[:], T.lo32[:, 0:1], 2048.0, mult, mult).then_inc(S.s_dla, 1)
-    V.tensor_scalar(T.dlo[:, 128:256], T.id16[:], T.lo32[:, 1:2], 2048.0, mult, mult).then_inc(S.s_dlb, 1)
+    V.tensor_scalar(T.dlo[:, 0:128], T.idr[:], T.lo32[:, 0:1], 2048.0, mult, mult).then_inc(S.s_dla, 1)
+    V.tensor_scalar(T.dlo[:, 128:256], T.idr[:], T.lo32[:, 1:2], 2048.0, mult, mult).then_inc(S.s_dlb, 1)
+
+    bc = [T.bc0, T.bc1, T.bc2, T.bc3]
+    sb = [S.s_b0, S.s_b1, S.s_b2, S.s_b3]
+
+    def hi_pass(q):
+        P.matmul(bc[q][:, 0:64], T.c16[:], T.dhi[:, 64 * q:64 * q + 64], True, False)
+
+    def lo_pass(q):
+        P.matmul(bc[q][:, 0:64], T.eps16[:], T.dlo[:, 64 * q:64 * q + 64], False, True).then_inc(sb[q], 1)
 
     P.wait_ge(S.c_k, 3)
     P.wait_ge(S.s_dha, 1)
-    P.matmul(T.bc0[:, 0:128], T.c16[:], T.dhi[:, 0:128], True, False)
+    hi_pass(0)
+    hi_pass(1)
     P.wait_ge(S.s_dhb, 1)
-    P.matmul(T.bc1[:, 0:128], T.c16[:], T.dhi[:, 128:256], True, False)
+    hi_pass(2)
     P.wait_ge(S.s_dla, 1)
-    P.matmul(T.bc0[:, 0:128], T.eps16[:], T.dlo[:, 0:128], False, True).then_inc(S.s_b0, 1)
+    lo_pass(0)
+    lo_pass(1)
+    hi_pass(3)
     P.wait_ge(S.s_dlb, 1)
-    P.matmul(T.bc1[:, 0:128], T.eps16[:], T.dlo[:, 128:256], False, True).then_inc(S.s_b1, 1)
+    lo_pass(2)
+    lo_pass(3)
 
     V.wait_ge(S.s_xn, 1)
-    V.wait_ge(S.s_b0, 1)
-    V.tensor_tensor(T.ys[:, 0:128], T.xn[:, 0:128], T.bc0[:, 0:128], mult).then_inc(S.s_y0, 1)
-    V.wait_ge(S.s_b1, 1)
-    V.tensor_tensor(T.ys[:, 128:256], T.xn[:, 128:256], T.bc1[:, 0:128], mult).then_inc(S.s_y1, 1)
-    Q.wait_ge(S.s_y0, 1)
+    for q in range(4):
+        V.wait_ge(sb[q], 1)
+        V.tensor_tensor(T.ys[:, 64 * q:64 * q + 64], T.xn[:, 64 * q:64 * q + 64], bc[q][:, 0:64],
+                        mult).then_inc(S.s_y0 if q < 2 else S.s_y1, 1)
+    Q.wait_ge(S.s_y0, 2)
     Q.dma_start(T.y[:, 0:128], T.ys[:, 0:128]).then_inc(S.st, 16)
-    A.wait_ge(S.s_y1, 1)
+    A.wait_ge(S.s_y1, 2)
     A.dma_start(T.y[:, 128:256], T.ys[:, 128:256]).then_inc(S.st, 16)
-    g.wait_ge(S.lsem, 3 * E)
+    g.wait_ge(S.lsem, 5 * E)
     g.wait_ge(S.st, 32)

from concourse.bass import DstId, RemoteDMATransfer
from concourse.mybir import AluOpType, AxisListType, ActivationFunctionType

E = 8
SIM_CORES = 512

SCRATCH = {
    "xs": ("sbuf", [128, 256], "float32"),
    "xn": ("sbuf", [128, 256], "float32"),
    "ys": ("sbuf", [128, 256], "float32"),
    "rs": ("sbuf", [128, 1], "float32"),
    "ri": ("sbuf", [128, 1], "float32"),
    "one32": ("sbuf", [128, 128], "float32"),
    "oneb": ("sbuf", [128, 128], "bfloat16"),
    "idm": ("sbuf", [128, 128], "bfloat16"),
    "idh": ("sbuf", [128, 64], "bfloat16"),
    "idr": ("sbuf", [128, 128], "bfloat16"),
    "c16": ("sbuf", [128, 128], "float16"),
    "eps16": ("sbuf", [128, 128], "float16"),
    "kin": ("sbuf", [128, 4], "float32"),
    "sumb": ("sbuf", [128, 16], "float32"),
    "junk": ("sbuf", [128, 8], "float32"),
    "s2": ("sbuf", [128, 2], "float32"),
    "si32": ("sbuf", [128, 2], "float32"),
    "hi16": ("sbuf", [128, 2], "float16"),
    "lo32": ("sbuf", [128, 2], "float32"),
    "dhi": ("sbuf", [128, 256], "float16"),
    "dlo": ("sbuf", [128, 256], "float16"),
    "pss": ("psum", [128, 512], "float32"),
    "bc0": ("psum", [128, 512], "float32"),
    "bc1": ("psum", [128, 512], "float32"),
    "bc2": ("psum", [128, 512], "float32"),
    "bc3": ("psum", [128, 512], "float32"),
}
SEMAPHORES = ["ld", "c_one", "c_ob", "c_id", "c_k", "c_idh", "c_idr", "s_rs", "s_ri", "s_mm", "s_v", "s_xn", "arr",
              "a_rp", "lsem", "s_S", "s_si", "s_hi", "s_lo", "s_dha", "s_dhb", "s_dla", "s_dlb", "s_b0", "s_b1",
              "s_b2", "s_b3", "s_y0", "s_y1", "st"]

_PLAN = {}


def _low_bits(mask, n):
    out, b = 0, 1
    while n > 0:
        if mask & b:
            out |= b
            n -= 1
        b <<= 1
    return out


def _plan(T, topo):
    if _PLAN:
        return _PLAN
    ranks = list(T.cores)
    rackp, cablep, helper, serves = {}, {}, {}, {}
    for c in ranks:
        peers = [d for d in ranks if d != c and topo.may_write(c, d)]
        rackp[c] = [d for d in peers if topo.same_plane(c, d)][0]
        cablep[c] = [d for d in peers if not topo.same_plane(c, d)][0]
    for c in ranks:
        hosts = (topo.host(c), topo.host(rackp[c]))
        dests = [d for d in ranks if topo.host(d) in hosts and not topo.may_write(c, d) and d != c]
        k = [k for k in range(SIM_CORES)
             if topo.host(k) == topo.host(c) and topo.chip(k) == topo.chip(c) and k not in ranks
             and topo.die(k) == topo.die(c) and all(topo.may_write(k, d) for d in dests)][0]
        helper[c] = k
        serves[k] = [(d, 0 if topo.host(d) == topo.host(c) else 1) for d in dests]
    _PLAN.update(rackp=rackp, cablep=cablep, helper=helper, serves=serves)
    return _PLAN


def _transfer(core, topo, mask, dests, srcs, dsts, sem):
    ids = []
    for d in dests:
        rid, pid = topo.addr(d, core)
        ids.append(DstId(rid=rid, pnc=pid))
    return RemoteDMATransfer(dst_ids=ids, dma_engine_mask=mask, remote_sem=sem, srcs=srcs, dsts=dsts,
                             alu_op=1 if len(srcs) > 1 else 0)


def rank_program(g, core, T, topo):
    plan = _plan(T, topo)
    S = T.sem
    V, A, P, Q = g.vector, g.scalar, g.tensor, g.sync
    mult, add, sub = AluOpType.mult, AluOpType.add, AluOpType.subtract
    X, Copy = AxisListType.X, ActivationFunctionType.Copy

    if core in plan["serves"]:
        pairs = plan["serves"][core]
        far = ~0
        for d, _ in pairs:
            far &= topo.mask(core, d)
        far = _low_bits(far, E)
        g.wait_ge(S.c_idh, E)
        g.remote_dma_fused([_transfer(core, topo, far, [d for d, sl in pairs if sl == 0], [T.idh[:]],
                                      [T.idr[:, 0:64]], S.c_idr)], local_sem=S.lsem)
        g.wait_ge(S.arr, E)
        g.wait_ge(S.a_rp, E)
        g.remote_dma_fused([_transfer(core, topo, far, [d for d, _ in pairs], [T.kin[:]],
                                      [T.sumb[:, 4 * sl:4 * sl + 4] for _, sl in pairs], S.arr)], local_sem=S.lsem)
        g.wait_ge(S.lsem, 2 * E)
        return
    if T.rank_of(core) is None:
        return
    own, from_rp, from_cp = T.sumb[:, 12:14], T.sumb[:, 8:10], T.sumb[:, 10:12]
    my_helper, rackp, cablep = plan["helper"][core], plan["rackp"][core], plan["cablep"][core]
    cable_helper = plan["helper"][cablep]
    far = topo.mask(core, cable_helper) & topo.mask(core, rackp) & topo.mask(core, cablep)
    near = _low_bits(topo.mask(core, my_helper) & ~far, E)
    far = _low_bits(far, E)

    Q.dma_start(T.xs[:], T.x[:]).then_inc(S.ld, 16)

    V.memset(T.oneb[:], 1.0).then_inc(S.c_ob, 1)
    g.wait_ge(S.c_ob, 1)
    g.affine_select(T.idm[:], T.oneb[:], [[-1, 128]], AluOpType.is_equal, 0.0, 0, 1).then_inc(S.c_id, 1)
    g.wait_ge(S.c_id, 1)
    g.remote_dma_fused([_transfer(core, topo, near, [my_helper], [T.idm[:, 0:64]], [T.idh[:]], S.c_idh),
                        _transfer(core, topo, far, [rackp], [T.idm[:, 64:128]], [T.idr[:, 64:128]], S.c_idr)],
                       local_sem=S.lsem)
    V.memset(T.one32[:], 1.0).then_inc(S.c_one, 1)
    V.memset(T.sumb[:, 14:16], 0.0).then_inc(S.c_k, 1)
    V.wait_ge(S.c_one, 1)
    V.tensor_scalar(T.c16[:], T.one32[:], 16.0, None, mult).then_inc(S.c_k, 1)
    V.tensor_scalar(T.eps16[:], T.one32[:], 2.0 ** -7, None, mult).then_inc(S.c_k, 1)

    V.wait_ge(S.ld, 16)
    V.tensor_reduce(T.rs[:], T.xs[:], X, add).then_inc(S.s_rs, 1)
    V.wait_ge(S.s_rs, 1)
    V.reciprocal(T.ri[:], T.rs[:]).then_inc(S.s_ri, 1)
    P.wait_ge(S.ld, 16)
    P.wait_ge(S.s_ri, 1)
    P.matmul(T.pss[:, 0:1], T.xs[:, 0:128], T.ri[:], True, True).then_inc(S.s_mm, 1)
    P.matmul(T.pss[:, 1:2], T.xs[:, 128:256], T.ri[:], True, True).then_inc(S.s_mm, 1)
    V.wait_ge(S.s_mm, 2)
    V.tensor_scalar(own, T.pss[:, 0:2], 16.0, None, mult).then_inc(S.s_v, 1)

    g.wait_ge(S.s_v, 1)
    g.remote_dma_fused([_transfer(core, topo, near, [my_helper], [own], [T.kin[:, 0:2]], S.arr),
                        _transfer(core, topo, far, [cable_helper, rackp], [own], [T.kin[:, 2:4], from_rp], S.a_rp)],
                       local_sem=S.lsem)
    g.wait_ge(S.a_rp, E)
    g.remote_dma_fused([_transfer(core, topo, far, [cablep], [own, from_rp], [from_cp], S.arr)], local_sem=S.lsem)

    A.wait_ge(S.ld, 16)
    A.wait_ge(S.s_ri, 1)
    A.activation(T.xn[:], T.xs[:], Copy, scale=T.ri[:]).then_inc(S.s_xn, 1)

    V.wait_ge(S.c_k, 3)
    V.wait_ge(S.c_idr, 2 * E)
    V.wait_ge(S.s_v, 1)
    V.wait_ge(S.a_rp, E)
    V.wait_ge(S.arr, 3 * E)
    V.tensor_reduce(T.s2[:, 0:1], T.sumb[:, 0:16:2], X, add).then_inc(S.s_S, 1)
    A.wait_ge(S.c_k, 3)
    A.wait_ge(S.c_idr, 2 * E)
    A.wait_ge(S.s_v, 1)
    A.wait_ge(S.a_rp, E)
    A.wait_ge(S.arr, 3 * E)
    A.activation(T.junk[:], T.sumb[:, 1:16:2], Copy, accum_out=T.s2[:, 1:2]).then_inc(S.s_S, 1)
    V.wait_ge(S.s_S, 2)
    V.reciprocal(T.si32[:], T.s2[:]).then_inc(S.s_si, 1)

    V.wait_ge(S.s_si, 1)
    V.tensor_scalar(T.dhi[:, 0:128], T.idr[:], T.si32[:, 0:1], None, mult).then_inc(S.s_dha, 1)
    A.wait_ge(S.s_si, 1)
    A.activation(T.dhi[:, 128:256], T.idr[:], Copy, scale=T.si32[:, 1:2]).then_inc(S.s_dhb, 1)
    V.tensor_copy(T.hi16[:], T.si32[:]).then_inc(S.s_hi, 1)
    V.wait_ge(S.s_hi, 1)
    V.tensor_tensor(T.lo32[:], T.si32[:], T.hi16[:], sub).then_inc(S.s_lo, 1)
    V.wait_ge(S.s_lo, 1)
    V.tensor_scalar(T.dlo[:, 0:128], T.idr[:], T.lo32[:, 0:1], 2048.0, mult, mult).then_inc(S.s_dla, 1)
    V.tensor_scalar(T.dlo[:, 128:256], T.idr[:], T.lo32[:, 1:2], 2048.0, mult, mult).then_inc(S.s_dlb, 1)

    bc = [T.bc0, T.bc1, T.bc2, T.bc3]
    sb = [S.s_b0, S.s_b1, S.s_b2, S.s_b3]

    def hi_pass(q):
        P.matmul(bc[q][:, 0:64], T.c16[:], T.dhi[:, 64 * q:64 * q + 64], True, False)

    def lo_pass(q):
        P.matmul(bc[q][:, 0:64], T.eps16[:], T.dlo[:, 64 * q:64 * q + 64], False, True).then_inc(sb[q], 1)

    P.wait_ge(S.c_k, 3)
    P.wait_ge(S.s_dha, 1)
    hi_pass(0)
    hi_pass(1)
    P.wait_ge(S.s_dhb, 1)
    hi_pass(2)
    P.wait_ge(S.s_dla, 1)
    lo_pass(0)
    lo_pass(1)
    hi_pass(3)
    P.wait_ge(S.s_dlb, 1)
    lo_pass(2)
    lo_pass(3)

    V.wait_ge(S.s_xn, 1)
    for q in range(4):
        V.wait_ge(sb[q], 1)
        V.tensor_tensor(T.ys[:, 64 * q:64 * q + 64], T.xn[:, 64 * q:64 * q + 64], bc[q][:, 0:64],
                        mult).then_inc(S.s_y0 if q < 2 else S.s_y1, 1)
    Q.wait_ge(S.s_y0, 2)
    Q.dma_start(T.y[:, 0:128], T.ys[:, 0:128]).then_inc(S.st, 16)
    A.wait_ge(S.s_y1, 2)
    A.dma_start(T.y[:, 128:256], T.ys[:, 128:256]).then_inc(S.st, 16)
    g.wait_ge(S.lsem, 5 * E)
    g.wait_ge(S.st, 32)
